import numpy as np
CORES = [6,7,14,15,22,23,30,31,38,39,46,47,54,55,62,63]
N = 16
GROUPS = [[0,1],[2,3],[4,5],[6,7],[8,9],[10,11],[12,13],[14,15]]
def setup_inputs(rng):
    return {"x": rng.standard_normal((N, 128, 4), dtype=np.float32)}
def reference(x):
    y = np.empty((N, 128, 8), x.dtype)
    for g in GROUPS:
        s = np.concatenate([x[r] for r in g], axis=1)
        for r in g:
            y[r] = s
    return {"y": y}

W = 4

SCRATCH = {
    "stage": ("dram", [128, W], "float32"),
    "land": ("dram", [2, 128, W], "float32"),
}
SEMAPHORES = ["loaded", "sent", "arrived", "own", "stored"]


def rank_program(g, core, T, topo):
    rank = T.rank_of(core)
    if rank is None:
        return
    group = [grp for grp in T.tables["GROUPS"] if rank in grp][0]
    me = group.index(rank)
    peers = [(j, T.cores[r]) for j, r in enumerate(group) if r != rank]

    g.sync.dma_start(T.stage[:], T.x[:]).then_inc(T.sem.loaded, 16)
    g.sync.dma_start(T.y[:, me * W:(me + 1) * W], T.x[:]).then_inc(T.sem.own, 16)

    g.wait_ge(T.sem.loaded, 16)
    for _j, dst in peers:
        rid, pid, _se = topo.addr(dst)
        g.remote_dma(T.land[me], T.stage[:], T.sem.arrived, T.sem.sent, pid, rid, topo.mask(core, dst))
    g.wait_ge(T.sem.sent, 16 * len(peers))

    g.sync.wait_ge(T.sem.arrived, 16 * len(peers))
    for j, _dst in peers:
        g.sync.dma_start(T.y[:, j * W:(j + 1) * W], T.land[j]).then_inc(T.sem.stored, 16)
    g.sync.wait_ge(T.sem.stored, 16 * len(peers))
    g.sync.wait_ge(T.sem.own, 16)
